import numpy as np
import ml_dtypes


def mxq(x, axis, fmt="e4m3"):
    dtype, down = {"e4m3": (ml_dtypes.float8_e4m3fn, 7), "e5m2": (ml_dtypes.float8_e5m2, 14)}[fmt]
    v = np.moveaxis(np.asarray(x, np.float32).astype(ml_dtypes.bfloat16).astype(np.float64), axis, -1)
    blocks = v.reshape(v.shape[:-1] + (-1, 32))
    amax = np.abs(blocks).max(-1, keepdims=True)
    byte = np.maximum(np.where(amax > 0, np.frexp(amax)[1] - 1 + 127, 0) - down, 1)
    scale = np.exp2(byte - 127.0)
    codes = (blocks / scale).astype(np.float32).astype(dtype).astype(np.float64)
    return np.moveaxis((codes * scale).reshape(v.shape), -1, axis)


WIDE = False


def mx_kscale(k):
    if not WIDE:
        return np.ones(k)
    levels = np.array([10, -10, 5, -5, 0])
    if k % 512:
        return np.exp2(np.random.permutation(np.resize(levels, k // 32))).repeat(32)
    a = np.empty((k // 512, 16))
    for p in range(k // 512):
        a[p, :8] = np.random.permutation(np.resize(levels, 8))
        for g in range(8):
            far = levels[np.abs(levels - a[p, g]) >= 10]
            a[p, g + 8] = far[np.random.randint(len(far))]
    return np.exp2(a.ravel()).repeat(32)


def f64(x):
    return np.asarray(x).astype(np.float64)


def striped(idx):
    return np.tile(idx.reshape(-1, 16).T, (8, 1)).astype(np.uint16)


def unstriped(offs):
    return offs[:16].T.reshape(-1).astype(np.int64)


def pack_weight(w):
    k, n = w.shape
    w = f64(np.asarray(w, np.float32).astype(ml_dtypes.bfloat16)).reshape(k // 32, 32, n)
    amax = np.abs(w).max(1)
    byte = np.clip(np.where(amax > 0, np.frexp(amax)[1] - 1 + 127 - 7, 1), 1, 254)
    scaled = (w * np.exp2(127.0 - byte)[:, None, :]).reshape(k, n).astype(np.float32)
    words = np.ascontiguousarray(scaled.reshape(k // 512, 128, 4, n).transpose(0, 1, 3, 2)).astype(ml_dtypes.float8_e4m3fn).view(np.uint8)
    return words, np.ascontiguousarray(byte.astype(np.uint8).reshape(k // 512, 16, n))


def unpack_weight(words, scales):
    g, p, n, _ = words.shape
    vals = np.ascontiguousarray(words).view(ml_dtypes.float8_e4m3fn).astype(np.float64) * np.repeat(np.exp2(scales.astype(np.float64) - 127.0), 8, axis=1)[..., None]
    return vals.transpose(0, 1, 3, 2).reshape(g * 512, n)


def sigmoid(v):
    return 1.0 / (1.0 + np.exp(-np.maximum(v, -700.0)))


K, T, S, D, N, V = 1024, 4096, 1024, 4, 128, 256
P = 2 ** 7


def setup_inputs():
    n = np.random.standard_normal
    s = mx_kscale(K)[:, None]
    packed_xT = pack_weight(n((K, T)) * s)
    return {
        "x_words": packed_xT[0],
        "x_scales": packed_xT[1],
        "w1": (n((K, N)) / np.sqrt(K) / s).astype(np.float32),
        "w2": (n((K, N)) / np.sqrt(K) / s).astype(np.float32),
        "depth": (np.tile(np.random.uniform(0.2, 2.0, S), (P, 1))).astype(np.float32),
        "back": (n((N, V))).astype(np.float32),
        "offs": striped(np.random.permutation(T)[:S]),
    }


def reference(x_words, x_scales, w1, w2, depth, back, offs):
    xq = unpack_weight(x_words, x_scales)[:, unstriped(offs)]
    a = 0.95 * (sigmoid(mxq(f64(w2), 0, "e4m3").T @ xq))
    ww = a * f64(depth)[:1]
    col = mxq(f64(w1), 0, "e4m3").T @ xq
    cw = ww * col
    den = ww.reshape(len(ww), -1, D).sum(axis=2) + 0.05
    avg = (cw.reshape(len(cw), -1, D).sum(axis=2)) / den
    lt = np.log(-1.0 * a + 1.0)
    tr = np.exp(lt.reshape(len(lt), -1, D).sum(axis=2))
    return avg - (avg * tr) + f64(back) * tr

@@ -1,0 +1,186 @@
+from contextlib import ExitStack
+
+import concourse.mybir as mybir
+from concourse.masks import make_identity
+
+K, T, S, D, N, V = 1024, 4096, 1024, 4, 128, 256
+FLOPS = 2 * 2 * K * N * S
+BYTES = K * T + (K // 32) * T + 2 * K * N * 4 + S * 4 + 2 * N * V * 4 + 128 * (S // 16) * 2
+
+F32 = mybir.dt.float32
+BF16 = mybir.dt.bfloat16
+I32 = mybir.dt.int32
+U32 = mybir.dt.uint32
+U16 = mybir.dt.uint16
+U8 = mybir.dt.uint8
+FP8X4 = mybir.dt.float8_e4m3fn_x4
+ACT = mybir.ActivationFunctionType
+ALU = mybir.AluOpType
+AX = mybir.AxisListType
+
+P = 128
+PACK = 4
+PASSES = K // (P * PACK)
+HALVES = 2
+SH = S // HALVES
+VH = V // HALVES
+
+
+def tile_picked_yoit_over_p_kernel(tc, x_words, x_scales, w1, w2, depth, back, offs, out):
+    nc = tc.nc
+    with ExitStack() as ctx:
+        keep = ctx.enter_context(tc.tile_pool(name="keep", bufs=1))
+        psum = ctx.enter_context(tc.psum_pool(name="psum", bufs=1))
+
+        offsets = keep.tile([P, S // 16], U16, name="offsets")
+        nc.sync.dma_start(offsets[:], offs)
+
+        scale_table = keep.tile([P, T], U8, name="scale_table", align_bytes=64)
+        nc.vector.memset(scale_table[:].bitcast(I32), 0)
+
+        warm = keep.tile([P, 2], F32, name="warm")
+        nc.gpsimd.memset(warm[:, 0:1], 0.0)
+        nc.scalar.activation(warm[:, 1:2], warm[:, 0:1], ACT.Sigmoid)
+
+        def load_weight(w, o, name):
+            raw = keep.tile([P, PACK, N], F32, name=name)
+            nc.sync.dma_start(raw[:], w[512 * o : 512 * (o + 1), :].rearrange("(p j) m -> p j m", j=PACK))
+            return raw
+
+        for q in range(4):
+            nc.gpsimd.dma_start(scale_table[32 * q : 32 * q + 8, :].bitcast(I32), x_scales[:, 4 * q : 4 * q + 4, :].bitcast(I32))
+
+        def load_words(o):
+            table = keep.tile([P, T], I32, name="word_table%d" % o, align_bytes=64)
+            nc.sync.dma_start(table[:], x_words[o].rearrange("p n t -> p (n t)").bitcast(I32))
+            return table
+
+        word_tables = [load_words(0)]
+        depth_cols = keep.tile([P, HALVES, D], F32, name="depth_cols")
+        nc.sync.dma_start(depth_cols[:], depth[0, :].rearrange("(h v d) -> v h d", h=HALVES, d=D))
+        w2_raw = keep.tile([P, PASSES, PACK, N], F32, name="w2_raw")
+        nc.sync.dma_start(w2_raw[:], w2.rearrange("(o p j) m -> p o j m", o=PASSES, j=PACK))
+        word_tables.append(load_words(1))
+
+        w1_raw = [load_weight(w1, o, "w1_raw%d" % o) for o in range(PASSES)]
+        back_sb = keep.tile([P, V], F32, name="back_sb")
+        nc.sync.dma_start(back_sb[:], back)
+
+        ident = keep.tile([P, P], F32, name="ident")
+        make_identity(nc, ident[:])
+
+        x_scale = keep.tile([P, S], U8, name="x_scale", align_bytes=64)
+        nc.vector.tensor_copy(x_scale[:], scale_table[:].indirect(offsets[:]))
+
+        def quantise(raws, name, codes_tag):
+            grouped = keep.tile([P, PASSES, N, PACK], BF16, name=name + "_bf16", align_bytes=64)
+            for o in range(PASSES):
+                nc.scalar.copy(grouped[:, o], raws[o].rearrange("p j m -> p m j"))
+            codes = keep.tile([P, PASSES * N], U32, name=name + "_codes", tag=codes_tag, align_bytes=64)
+            scales = keep.tile([P, PASSES * N], U8, name=name + "_scales", align_bytes=64)
+            nc.vector.quantize_mx(out=codes[:].bitcast(FP8X4), scales=scales[:], in_=grouped[:].rearrange("p o m j -> p (o m j)"))
+            return codes, scales
+
+        w2_q = quantise([w2_raw[:, o] for o in range(PASSES)], "w2", "w2_codes")
+
+        depth_scaled = keep.tile([P, HALVES * D], F32, name="depth_scaled")
+        nc.vector.tensor_scalar(depth_scaled[:], depth_cols[:].rearrange("p h d -> p (h d)"), 0.95, None, ALU.mult)
+        depth_ps = []
+        for h in range(HALVES):
+            bank = psum.tile([P, D, VH], F32, name="depth_ps%d" % h)
+            for d in range(D):
+                c = h * D + d
+                nc.tensor.transpose(bank[:, d, :], depth_scaled[:, c : c + 1].to_broadcast([P, P]), ident[:])
+            depth_ps.append(bank)
+
+        x0 = keep.tile([P, S], U32, name="x0", align_bytes=64)
+        nc.vector.tensor_copy(x0[:], word_tables[0][:].bitcast(U32).indirect(offsets[:]))
+        x1 = [
+            keep.tile([P, SH], U32, name="x1_0", tag="scale_table", align_bytes=64),
+            keep.tile([P, SH], U32, name="x1_1", align_bytes=64),
+        ]
+
+        def product(bank, wq, o, h):
+            codes, scales = wq
+            cols = slice(h * SH, (h + 1) * SH)
+            moving = x0[:, cols] if o == 0 else x1[h][:]
+            nc.tensor.matmul_mx(
+                out=bank[:],
+                lhsT=codes[:, o * N : (o + 1) * N].bitcast(FP8X4),
+                lhsT_scale=scales[:, o * N : (o + 1) * N],
+                rhs=moving.bitcast(FP8X4),
+                rhs_scale=x_scale[4 * o : P, cols],
+                start=(o == 0),
+                stop=(o == PASSES - 1),
+            )
+
+        z_ps = [psum.tile([P, SH], F32, name="z_ps%d" % h) for h in range(HALVES)]
+        col_ps = [psum.tile([P, SH], F32, name="col_ps%d" % h) for h in range(HALVES)]
+        for h in range(HALVES):
+            product(z_ps[h], w2_q, 0, h)
+
+        sig, passing = [], []
+        for h in range(HALVES):
+            nc.vector.tensor_copy(x1[h][:], word_tables[1][:].bitcast(U32).indirect(offsets[:, h * SH // 16 : (h + 1) * SH // 16]))
+            product(z_ps[h], w2_q, 1, h)
+        w1_q = quantise([r[:] for r in w1_raw], "w1", "word_table1")
+        for h in range(HALVES):
+            s = keep.tile([P, D, VH], F32, name="sig%d" % h)
+            nc.scalar.activation(s[:], z_ps[h][:].rearrange("p (v d) -> p d v", d=D), ACT.Sigmoid)
+            sig.append(s)
+        for h in range(HALVES):
+            for o in range(PASSES):
+                product(col_ps[h], w1_q, o, h)
+        tr = keep.tile([P, V], F32, name="tr")
+        for h in range(HALVES):
+            u = keep.tile([P, D, VH], F32, name="u%d" % h)
+            if h == 0:
+                nc.scalar.activation(u[:], sig[h][:], ACT.Copy, scale=-0.95, bias=1.0)
+            else:
+                nc.gpsimd.tensor_scalar(u[:], sig[h][:], -0.95, 1.0, ALU.mult, ALU.add)
+            pair = keep.tile([P, 2, VH], F32, name="pair%d" % h)
+            nc.gpsimd.tensor_tensor(pair[:], u[:, 0:2, :], u[:, 2:4, :], ALU.mult)
+            nc.gpsimd.tensor_tensor(tr[:, h * VH : (h + 1) * VH], pair[:, 0, :], pair[:, 1, :], ALU.mult)
+        bt = keep.tile([P, V], F32, name="bt")
+        nc.gpsimd.tensor_tensor(bt[:], tr[:], back_sb[:], ALU.mult)
+
+        def sum_turned(bank, terms):
+            for d in range(D):
+                nc.tensor.matmul(bank, lhsT=terms[:, d, :], rhs=ident[:], is_transpose=True, start=(d == 0), stop=(d == D - 1))
+
+        ww = [keep.tile([P, D, VH], F32, name="ww%d" % h) for h in range(HALVES)]
+        cw = [keep.tile([P, D, VH], F32, name="cw%d" % h) for h in range(HALVES)]
+        den_ps = psum.tile([P, HALVES, N], F32, name="den_ps")
+        for h in range(HALVES):
+            nc.vector.tensor_tensor(ww[h][:], sig[h][:], depth_ps[h][:], ALU.mult)
+            sum_turned(den_ps[:, h, :], ww[h])
+        num_ps = []
+        for h in range(HALVES):
+            nc.vector.tensor_tensor(cw[h][:], ww[h][:], col_ps[h][:].rearrange("p (v d) -> p d v", d=D), ALU.mult)
+            bank = psum.tile([P, N], F32, name="num_ps%d" % h, tag="depth_ps%d" % h)
+            sum_turned(bank[:], cw[h])
+            num_ps.append(bank)
+
+        root = keep.tile([P, HALVES, N], F32, name="root")
+        nc.scalar.activation(root[:], den_ps[:], ACT.Abs_reciprocal_sqrt, bias=0.05)
+        inv_abs = keep.tile([P, HALVES, N], F32, name="inv_abs")
+        nc.scalar.activation(inv_abs[:], root[:], ACT.Square)
+        side = keep.tile([P, HALVES, N], F32, name="side")
+        nc.vector.tensor_scalar(side[:], den_ps[:], -0.05, 2.0, ALU.is_ge, ALU.mult)
+        inv = keep.tile([P, HALVES, N], F32, name="inv")
+        nc.vector.scalar_tensor_tensor(inv[:], side[:], 1.0, inv_abs[:], ALU.subtract, ALU.mult)
+
+        avg_ps = []
+        for h in range(HALVES):
+            avg_t = keep.tile([P, N], F32, name="avg_t%d" % h)
+            nc.vector.tensor_tensor(avg_t[:], inv[:, h, :], num_ps[h][:], ALU.mult)
+            bank = psum.tile([P, VH], F32, name="avg_ps%d" % h, tag="z_ps%d" % h)
+            nc.tensor.transpose(bank[:], avg_t[:], ident[:])
+            avg_ps.append(bank)
+        hidden = [keep.tile([P, VH], F32, name="hidden%d" % h) for h in range(HALVES)]
+        for h in range(HALVES):
+            nc.vector.scalar_tensor_tensor(hidden[h][:], tr[:, h * VH : (h + 1) * VH], 1.0, avg_ps[h][:], ALU.subtract, ALU.mult)
+        for h in range(HALVES):
+            res = keep.tile([P, VH], F32, name="res%d" % h)
+            nc.vector.tensor_tensor(res[:], bt[:, h * VH : (h + 1) * VH], hidden[h][:], ALU.subtract)
+            nc.sync.dma_start(out[:, h * VH : (h + 1) * VH], res[:])

@@ -42,13 +42,15 @@ def tile_picked_yoit_over_p_kernel(tc, x_words, x_scales, w1, w2, depth, back, o
         nc.gpsimd.memset(warm[:, 0:1], 0.0)
         nc.scalar.activation(warm[:, 1:2], warm[:, 0:1], ACT.Sigmoid)
 
-        def load_weight(w, o, name):
-            raw = keep.tile([P, PACK, N], F32, name=name)
+        depth_cols = keep.tile([P, HALVES, D], F32, name="depth_cols")
+        nc.sync.dma_start(depth_cols[:], depth[0, :].rearrange("(h v d) -> v h d", h=HALVES, d=D))
+
+        def load_weight(w, o, name, tag):
+            raw = keep.tile([P, PACK, N], F32, name=name, tag=tag, align_bytes=64)
             nc.sync.dma_start(raw[:], w[512 * o : 512 * (o + 1), :].rearrange("(p j) m -> p j m", j=PACK))
             return raw
 
-        for q in range(4):
-            nc.gpsimd.dma_start(scale_table[32 * q : 32 * q + 8, :].bitcast(I32), x_scales[:, 4 * q : 4 * q + 4, :].bitcast(I32))
+        w2_raw = [load_weight(w2, 0, "w2_raw0", "word_table1"), load_weight(w2, 1, "w2_raw1", "w2_raw1")]
 
         def load_words(o):
             table = keep.tile([P, T], I32, name="word_table%d" % o, align_bytes=64)
@@ -56,32 +58,29 @@ def tile_picked_yoit_over_p_kernel(tc, x_words, x_scales, w1, w2, depth, back, o
             return table
 
         word_tables = [load_words(0)]
-        depth_cols = keep.tile([P, HALVES, D], F32, name="depth_cols")
-        nc.sync.dma_start(depth_cols[:], depth[0, :].rearrange("(h v d) -> v h d", h=HALVES, d=D))
-        w2_raw = keep.tile([P, PASSES, PACK, N], F32, name="w2_raw")
-        nc.sync.dma_start(w2_raw[:], w2.rearrange("(o p j) m -> p o j m", o=PASSES, j=PACK))
-        word_tables.append(load_words(1))
-
-        w1_raw = [load_weight(w1, o, "w1_raw%d" % o) for o in range(PASSES)]
-        back_sb = keep.tile([P, V], F32, name="back_sb")
-        nc.sync.dma_start(back_sb[:], back)
+        for q in range(2):
+            nc.sync.dma_start(scale_table[32 * q : 32 * q + 8, :].bitcast(I32), x_scales[:, 4 * q : 4 * q + 4, :].bitcast(I32))
+        for q in range(2, 4):
+            for o in range(PASSES):
+                r0 = 32 * q + 4 * o
+                nc.sync.dma_start(scale_table[r0 : r0 + 4, :].bitcast(I32), x_scales[o, 4 * q : 4 * q + 4, :].bitcast(I32))
 
         ident = keep.tile([P, P], F32, name="ident")
         make_identity(nc, ident[:])
 
-        x_scale = keep.tile([P, S], U8, name="x_scale", align_bytes=64)
-        nc.vector.tensor_copy(x_scale[:], scale_table[:].indirect(offsets[:]))
-
-        def quantise(raws, name, codes_tag):
-            grouped = keep.tile([P, PASSES, N, PACK], BF16, name=name + "_bf16", align_bytes=64)
-            for o in range(PASSES):
-                nc.scalar.copy(grouped[:, o], raws[o].rearrange("p j m -> p m j"))
-            codes = keep.tile([P, PASSES * N], U32, name=name + "_codes", tag=codes_tag, align_bytes=64)
+        def quantise(raws, name):
+            codes = keep.tile([P, PASSES * N], U32, name=name + "_codes", align_bytes=64)
             scales = keep.tile([P, PASSES * N], U8, name=name + "_scales", align_bytes=64)
-            nc.vector.quantize_mx(out=codes[:].bitcast(FP8X4), scales=scales[:], in_=grouped[:].rearrange("p o m j -> p (o m j)"))
+            for o in range(PASSES):
+                grouped = keep.tile([P, N, PACK], BF16, name=name + "_bf16_%d" % o, align_bytes=64)
+                nc.scalar.copy(grouped[:], raws[o][:].rearrange("p j m -> p m j"))
+                cols = slice(o * N, (o + 1) * N)
+                nc.vector.quantize_mx(out=codes[:, cols].bitcast(FP8X4), scales=scales[:, cols], in_=grouped[:].rearrange("p m j -> p (m j)"))
             return codes, scales
 
-        w2_q = quantise([w2_raw[:, o] for o in range(PASSES)], "w2", "w2_codes")
+        w2_q = quantise(w2_raw, "w2")
+        word_tables.append(load_words(1))
+        w1_raw = [load_weight(w1, o, "w1_raw%d" % o, "w2_bf16_%d" % o) for o in range(PASSES)]
 
         depth_scaled = keep.tile([P, HALVES * D], F32, name="depth_scaled")
         nc.vector.tensor_scalar(depth_scaled[:], depth_cols[:].rearrange("p h d -> p (h d)"), 0.95, None, ALU.mult)
@@ -95,10 +94,11 @@ def tile_picked_yoit_over_p_kernel(tc, x_words, x_scales, w1, w2, depth, back, o
 
         x0 = keep.tile([P, S], U32, name="x0", align_bytes=64)
         nc.vector.tensor_copy(x0[:], word_tables[0][:].bitcast(U32).indirect(offsets[:]))
-        x1 = [
-            keep.tile([P, SH], U32, name="x1_0", tag="scale_table", align_bytes=64),
-            keep.tile([P, SH], U32, name="x1_1", align_bytes=64),
-        ]
+        x_scale = keep.tile([P, S], U8, name="x_scale", align_bytes=64)
+        nc.vector.tensor_copy(x_scale[:], scale_table[:].indirect(offsets[:]))
+        back_sb = keep.tile([P, V], F32, name="back_sb", tag="word_table0", align_bytes=64)
+        nc.sync.dma_start(back_sb[:], back)
+        x1 = [keep.tile([P, SH], U32, name="x1_%d" % h, align_bytes=64) for h in range(HALVES)]
 
         def product(bank, wq, o, h):
             codes, scales = wq
@@ -119,11 +119,11 @@ def tile_picked_yoit_over_p_kernel(tc, x_words, x_scales, w1, w2, depth, back, o
         for h in range(HALVES):
             product(z_ps[h], w2_q, 0, h)
 
-        sig, passing = [], []
+        sig = []
         for h in range(HALVES):
             nc.vector.tensor_copy(x1[h][:], word_tables[1][:].bitcast(U32).indirect(offsets[:, h * SH // 16 : (h + 1) * SH // 16]))
             product(z_ps[h], w2_q, 1, h)
-        w1_q = quantise([r[:] for r in w1_raw], "w1", "word_table1")
+        w1_q = quantise(w1_raw, "w1")
         for h in range(HALVES):
             s = keep.tile([P, D, VH], F32, name="sig%d" % h)
             nc.scalar.activation(s[:], z_ps[h][:].rearrange("p (v d) -> p d v", d=D), ACT.Sigmoid)
@@ -133,16 +133,11 @@ def tile_picked_yoit_over_p_kernel(tc, x_words, x_scales, w1, w2, depth, back, o
                 product(col_ps[h], w1_q, o, h)
         tr = keep.tile([P, V], F32, name="tr")
         for h in range(HALVES):
-            u = keep.tile([P, D, VH], F32, name="u%d" % h)
-            if h == 0:
-                nc.scalar.activation(u[:], sig[h][:], ACT.Copy, scale=-0.95, bias=1.0)
-            else:
-                nc.gpsimd.tensor_scalar(u[:], sig[h][:], -0.95, 1.0, ALU.mult, ALU.add)
+            u = keep.tile([P, D, VH], F32, name="u%d" % h, tag="u")
+            nc.gpsimd.tensor_scalar(u[:], sig[h][:], -0.95, 1.0, ALU.mult, ALU.add)
             pair = keep.tile([P, 2, VH], F32, name="pair%d" % h)
             nc.gpsimd.tensor_tensor(pair[:], u[:, 0:2, :], u[:, 2:4, :], ALU.mult)
             nc.gpsimd.tensor_tensor(tr[:, h * VH : (h + 1) * VH], pair[:, 0, :], pair[:, 1, :], ALU.mult)
-        bt = keep.tile([P, V], F32, name="bt")
-        nc.gpsimd.tensor_tensor(bt[:], tr[:], back_sb[:], ALU.mult)
 
         def sum_turned(bank, terms):
             for d in range(D):
@@ -151,10 +146,10 @@ def tile_picked_yoit_over_p_kernel(tc, x_words, x_scales, w1, w2, depth, back, o
         ww = [keep.tile([P, D, VH], F32, name="ww%d" % h) for h in range(HALVES)]
         cw = [keep.tile([P, D, VH], F32, name="cw%d" % h) for h in range(HALVES)]
         den_ps = psum.tile([P, HALVES, N], F32, name="den_ps")
+        num_ps = []
         for h in range(HALVES):
             nc.vector.tensor_tensor(ww[h][:], sig[h][:], depth_ps[h][:], ALU.mult)
             sum_turned(den_ps[:, h, :], ww[h])
-        num_ps = []
         for h in range(HALVES):
             nc.vector.tensor_tensor(cw[h][:], ww[h][:], col_ps[h][:].rearrange("p (v d) -> p d v", d=D), ALU.mult)
             bank = psum.tile([P, N], F32, name="num_ps%d" % h, tag="depth_ps%d" % h)
@@ -162,21 +157,25 @@ def tile_picked_yoit_over_p_kernel(tc, x_words, x_scales, w1, w2, depth, back, o
             num_ps.append(bank)
 
         root = keep.tile([P, HALVES, N], F32, name="root")
-        nc.scalar.activation(root[:], den_ps[:], ACT.Abs_reciprocal_sqrt, bias=0.05)
+        for h in range(HALVES):
+            nc.scalar.activation(root[:, h, :], den_ps[:, h, :], ACT.Abs_reciprocal_sqrt, bias=0.05)
         inv_abs = keep.tile([P, HALVES, N], F32, name="inv_abs")
-        nc.scalar.activation(inv_abs[:], root[:], ACT.Square)
+        for h in range(HALVES):
+            nc.scalar.activation(inv_abs[:, h, :], root[:, h, :], ACT.Square)
         side = keep.tile([P, HALVES, N], F32, name="side")
         nc.vector.tensor_scalar(side[:], den_ps[:], -0.05, 2.0, ALU.is_ge, ALU.mult)
-        inv = keep.tile([P, HALVES, N], F32, name="inv")
-        nc.vector.scalar_tensor_tensor(inv[:], side[:], 1.0, inv_abs[:], ALU.subtract, ALU.mult)
-
+        signed = keep.tile([P, HALVES, N], F32, name="signed")
+        for h in range(HALVES):
+            nc.vector.scalar_tensor_tensor(signed[:, h, :], side[:, h, :], 1.0, num_ps[h][:], ALU.subtract, ALU.mult)
         avg_ps = []
         for h in range(HALVES):
             avg_t = keep.tile([P, N], F32, name="avg_t%d" % h)
-            nc.vector.tensor_tensor(avg_t[:], inv[:, h, :], num_ps[h][:], ALU.mult)
+            nc.vector.tensor_tensor(avg_t[:], signed[:, h, :], inv_abs[:, h, :], ALU.mult)
             bank = psum.tile([P, VH], F32, name="avg_ps%d" % h, tag="z_ps%d" % h)
             nc.tensor.transpose(bank[:], avg_t[:], ident[:])
             avg_ps.append(bank)
+        bt = keep.tile([P, V], F32, name="bt", tag="inv_abs")
+        nc.vector.tensor_tensor(bt[:], tr[:], back_sb[:], ALU.mult)
         hidden = [keep.tile([P, VH], F32, name="hidden%d" % h) for h in range(HALVES)]
         for h in range(HALVES):
             nc.vector.scalar_tensor_tensor(hidden[h][:], tr[:, h * VH : (h + 1) * VH], 1.0, avg_ps[h][:], ALU.subtract, ALU.mult)

@@ -43,12 +43,12 @@ def tile_picked_yoit_over_p_kernel(tc, x_words, x_scales, w1, w2, depth, back, o
         nc.scalar.activation(warm[:, 1:2], warm[:, 0:1], ACT.Sigmoid)
 
         depth_cols = keep.tile([P, HALVES, D], F32, name="depth_cols")
-        nc.sync.dma_start(depth_cols[:], depth[0, :].rearrange("(h v d) -> v h d", h=HALVES, d=D))
+        nc.scalar.dma_start(depth_cols[:], depth[0, :].rearrange("(h v d) -> v h d", h=HALVES, d=D))
 
         def load_weight(w, o, name, tag):
             raw = keep.tile([P, PACK, N], F32, name=name, tag=tag, align_bytes=64)
             nc.sync.dma_start(raw[:], w[512 * o : 512 * (o + 1), :].rearrange("(p j) m -> p j m", j=PACK))
-            return raw
+            return raw[:]
 
         w2_raw = [load_weight(w2, 0, "w2_raw0", "word_table1"), load_weight(w2, 1, "w2_raw1", "w2_raw1")]
 
@@ -58,12 +58,8 @@ def tile_picked_yoit_over_p_kernel(tc, x_words, x_scales, w1, w2, depth, back, o
             return table
 
         word_tables = [load_words(0)]
-        for q in range(2):
-            nc.sync.dma_start(scale_table[32 * q : 32 * q + 8, :].bitcast(I32), x_scales[:, 4 * q : 4 * q + 4, :].bitcast(I32))
-        for q in range(2, 4):
-            for o in range(PASSES):
-                r0 = 32 * q + 4 * o
-                nc.sync.dma_start(scale_table[r0 : r0 + 4, :].bitcast(I32), x_scales[o, 4 * q : 4 * q + 4, :].bitcast(I32))
+        for o in range(PASSES):
+            nc.scalar.dma_start(scale_table[4 * o : P : 8, :].bitcast(I32), x_scales[o].bitcast(I32))
 
         ident = keep.tile([P, P], F32, name="ident")
         make_identity(nc, ident[:])
@@ -73,14 +69,16 @@ def tile_picked_yoit_over_p_kernel(tc, x_words, x_scales, w1, w2, depth, back, o
             scales = keep.tile([P, PASSES * N], U8, name=name + "_scales", align_bytes=64)
             for o in range(PASSES):
                 grouped = keep.tile([P, N, PACK], BF16, name=name + "_bf16_%d" % o, align_bytes=64)
-                nc.scalar.copy(grouped[:], raws[o][:].rearrange("p j m -> p m j"))
+                nc.scalar.copy(grouped[:], raws[o].rearrange("p j m -> p m j"))
                 cols = slice(o * N, (o + 1) * N)
                 nc.vector.quantize_mx(out=codes[:, cols].bitcast(FP8X4), scales=scales[:, cols], in_=grouped[:].rearrange("p m j -> p (m j)"))
             return codes, scales
 
         w2_q = quantise(w2_raw, "w2")
         word_tables.append(load_words(1))
-        w1_raw = [load_weight(w1, o, "w1_raw%d" % o, "w2_bf16_%d" % o) for o in range(PASSES)]
+        w1_both = keep.tile([P, PASSES, PACK, N], F32, name="w1_both", tag="w2_bf16_1", align_bytes=64)
+        nc.sync.dma_start(w1_both[:], w1.rearrange("(o p j) m -> p o j m", o=PASSES, j=PACK))
+        w1_raw = [w1_both[:, o] for o in range(PASSES)]
 
         depth_scaled = keep.tile([P, HALVES * D], F32, name="depth_scaled")
         nc.vector.tensor_scalar(depth_scaled[:], depth_cols[:].rearrange("p h d -> p (h d)"), 0.95, None, ALU.mult)
@@ -92,11 +90,16 @@ def tile_picked_yoit_over_p_kernel(tc, x_words, x_scales, w1, w2, depth, back, o
                 nc.tensor.transpose(bank[:, d, :], depth_scaled[:, c : c + 1].to_broadcast([P, P]), ident[:])
             depth_ps.append(bank)
 
-        x0 = keep.tile([P, S], U32, name="x0", align_bytes=64)
-        nc.vector.tensor_copy(x0[:], word_tables[0][:].bitcast(U32).indirect(offsets[:]))
+        picked_scales = keep.tile([P, S], U8, name="picked_scales", align_bytes=64)
+        nc.vector.tensor_copy(picked_scales[:], scale_table[:].indirect(offsets[:]))
         x_scale = keep.tile([P, S], U8, name="x_scale", align_bytes=64)
-        nc.vector.tensor_copy(x_scale[:], scale_table[:].indirect(offsets[:]))
-        back_sb = keep.tile([P, V], F32, name="back_sb", tag="word_table0", align_bytes=64)
+        nc.vector.tensor_copy(x_scale[:].bitcast(I32), picked_scales[:].bitcast(I32))
+        for o in range(PASSES):
+            for r in range(1, 4):
+                nc.scalar.dma_start(x_scale[4 * o + r : P : 32, :].bitcast(I32), picked_scales[8 * r + 4 * o : P : 32, :].bitcast(I32))
+        x0 = keep.tile([P, S], U32, name="x0", tag="scale_table", align_bytes=64)
+        nc.vector.tensor_copy(x0[:], word_tables[0][:].bitcast(U32).indirect(offsets[:]))
+        back_sb = keep.tile([P, V], F32, name="back_sb", tag="picked_scales", align_bytes=64)
         nc.sync.dma_start(back_sb[:], back)
         x1 = [keep.tile([P, SH], U32, name="x1_%d" % h, align_bytes=64) for h in range(HALVES)]
 
@@ -119,7 +122,9 @@ def tile_picked_yoit_over_p_kernel(tc, x_words, x_scales, w1, w2, depth, back, o
         for h in range(HALVES):
             product(z_ps[h], w2_q, 0, h)
 
-        sig = []
+        one = keep.tile([P, 1], F32, name="one", tag="sig1")
+        nc.gpsimd.memset(one[:], 1.0)
+        sig, passing = [], []
         for h in range(HALVES):
             nc.vector.tensor_copy(x1[h][:], word_tables[1][:].bitcast(U32).indirect(offsets[:, h * SH // 16 : (h + 1) * SH // 16]))
             product(z_ps[h], w2_q, 1, h)
@@ -128,13 +133,18 @@ def tile_picked_yoit_over_p_kernel(tc, x_words, x_scales, w1, w2, depth, back, o
             s = keep.tile([P, D, VH], F32, name="sig%d" % h)
             nc.scalar.activation(s[:], z_ps[h][:].rearrange("p (v d) -> p d v", d=D), ACT.Sigmoid)
             sig.append(s)
+            u = keep.tile([P, D, VH], F32, name="u%d" % h)
+            if h == 0:
+                nc.scalar.activation(u[:], s[:], ACT.Identity, scale=-0.95, bias=one[:])
+            passing.append(u)
         for h in range(HALVES):
             for o in range(PASSES):
                 product(col_ps[h], w1_q, o, h)
         tr = keep.tile([P, V], F32, name="tr")
         for h in range(HALVES):
-            u = keep.tile([P, D, VH], F32, name="u%d" % h, tag="u")
-            nc.gpsimd.tensor_scalar(u[:], sig[h][:], -0.95, 1.0, ALU.mult, ALU.add)
+            u = passing[h]
+            if h == 1:
+                nc.gpsimd.tensor_scalar(u[:], sig[h][:], -0.95, 1.0, ALU.mult, ALU.add)
             pair = keep.tile([P, 2, VH], F32, name="pair%d" % h)
             nc.gpsimd.tensor_tensor(pair[:], u[:, 0:2, :], u[:, 2:4, :], ALU.mult)
             nc.gpsimd.tensor_tensor(tr[:, h * VH : (h + 1) * VH], pair[:, 0, :], pair[:, 1, :], ALU.mult)

@@ -36,49 +36,66 @@ def tile_picked_yoit_over_p_kernel(tc, x_words, x_scales, w1, w2, depth, back, o
         nc.sync.dma_start(offsets[:], offs)
 
         scale_table = keep.tile([P, T], U8, name="scale_table", align_bytes=64)
-        nc.vector.memset(scale_table[:].bitcast(I32), 0)
+        nc.gpsimd.memset(scale_table[:, : T // 2].bitcast(I32), 0)
+        nc.vector.memset(scale_table[:, T // 2 :].bitcast(I32), 0)
 
         warm = keep.tile([P, 2], F32, name="warm")
         nc.gpsimd.memset(warm[:, 0:1], 0.0)
         nc.scalar.activation(warm[:, 1:2], warm[:, 0:1], ACT.Sigmoid)
 
         depth_cols = keep.tile([P, HALVES, D], F32, name="depth_cols")
-        nc.scalar.dma_start(depth_cols[:], depth[0, :].rearrange("(h v d) -> v h d", h=HALVES, d=D))
+        nc.sync.dma_start(depth_cols[:], depth[0, :].rearrange("(h v d) -> v h d", h=HALVES, d=D))
 
-        def load_weight(w, o, name, tag):
+        unit = keep.tile([P, 1], F32, name="unit", tag="word_table0", align_bytes=64)
+        nc.gpsimd.memset(unit[:], 1.0)
+        floor = keep.tile([P, 1], F32, name="floor")
+        nc.vector.tensor_scalar(floor[:], unit[:], 0.05, None, ALU.mult)
+
+        def load_weight(w, name, tag):
+            both = keep.tile([P, PASSES, PACK, N], F32, name=name, tag=tag, align_bytes=64)
+            nc.sync.dma_start(both[:], w.rearrange("(o p j) m -> p o j m", o=PASSES, j=PACK))
+            return [both[:, o] for o in range(PASSES)]
+
+        def load_pass(w, o, name, tag):
             raw = keep.tile([P, PACK, N], F32, name=name, tag=tag, align_bytes=64)
             nc.sync.dma_start(raw[:], w[512 * o : 512 * (o + 1), :].rearrange("(p j) m -> p j m", j=PACK))
             return raw[:]
 
-        w2_raw = [load_weight(w2, 0, "w2_raw0", "word_table1"), load_weight(w2, 1, "w2_raw1", "w2_raw1")]
+        w2_raw = load_weight(w2, "w2_both", "w2_both")
+        w1_raw1 = load_pass(w1, 1, "w1_raw1", "w1_raw1")
 
-        def load_words(o):
-            table = keep.tile([P, T], I32, name="word_table%d" % o, align_bytes=64)
+        for o in range(PASSES):
+            nc.sync.dma_start(scale_table[4 * o : P : 8, :].bitcast(I32), x_scales[o].bitcast(I32))
+
+        def load_words(o, tag):
+            table = keep.tile([P, T], I32, name="word_table%d" % o, tag=tag, align_bytes=64)
             nc.sync.dma_start(table[:], x_words[o].rearrange("p n t -> p (n t)").bitcast(I32))
             return table
 
-        word_tables = [load_words(0)]
-        for o in range(PASSES):
-            nc.scalar.dma_start(scale_table[4 * o : P : 8, :].bitcast(I32), x_scales[o].bitcast(I32))
+        word_tables = [load_words(0, "word_table0")]
 
         ident = keep.tile([P, P], F32, name="ident")
         make_identity(nc, ident[:])
 
-        def quantise(raws, name):
-            codes = keep.tile([P, PASSES * N], U32, name=name + "_codes", align_bytes=64)
-            scales = keep.tile([P, PASSES * N], U8, name=name + "_scales", align_bytes=64)
-            for o in range(PASSES):
-                grouped = keep.tile([P, N, PACK], BF16, name=name + "_bf16_%d" % o, align_bytes=64)
-                nc.scalar.copy(grouped[:], raws[o].rearrange("p j m -> p m j"))
-                cols = slice(o * N, (o + 1) * N)
-                nc.vector.quantize_mx(out=codes[:, cols].bitcast(FP8X4), scales=scales[:, cols], in_=grouped[:].rearrange("p m j -> p (m j)"))
+        def quantise(raw, name):
+            grouped = keep.tile([P, N, PACK], BF16, name=name + "_bf16", align_bytes=64)
+            nc.scalar.copy(grouped[:], raw.rearrange("p j m -> p m j"))
+            codes = keep.tile([P, N], U32, name=name + "_codes", align_bytes=64)
+            scales = keep.tile([P, N], U8, name=name + "_scales", align_bytes=64)
+            nc.vector.quantize_mx(out=codes[:].bitcast(FP8X4), scales=scales[:], in_=grouped[:].rearrange("p m j -> p (m j)"))
             return codes, scales
 
-        w2_q = quantise(w2_raw, "w2")
-        word_tables.append(load_words(1))
-        w1_both = keep.tile([P, PASSES, PACK, N], F32, name="w1_both", tag="w2_bf16_1", align_bytes=64)
-        nc.sync.dma_start(w1_both[:], w1.rearrange("(o p j) m -> p o j m", o=PASSES, j=PACK))
-        w1_raw = [w1_both[:, o] for o in range(PASSES)]
+        w2_q = [quantise(w2_raw[o], "w2_%d" % o) for o in range(PASSES)]
+        w1_q1 = quantise(w1_raw1, "w1_1")
+        word_tables.append(load_words(1, "w2_both"))
+
+        picked_scales = keep.tile([P, S], U8, name="picked_scales", align_bytes=64)
+        nc.vector.tensor_copy(picked_scales[:], scale_table[:].indirect(offsets[:]))
+        x_scale = keep.tile([P, S], U8, name="x_scale", align_bytes=64)
+        nc.vector.tensor_copy(x_scale[:].bitcast(I32), picked_scales[:].bitcast(I32))
+        for o in range(PASSES):
+            for r in range(1, 4):
+                nc.sync.dma_start(x_scale[4 * o + r : P : 32, :].bitcast(I32), picked_scales[8 * r + 4 * o : P : 32, :].bitcast(I32))
 
         depth_scaled = keep.tile([P, HALVES * D], F32, name="depth_scaled")
         nc.vector.tensor_scalar(depth_scaled[:], depth_cols[:].rearrange("p h d -> p (h d)"), 0.95, None, ALU.mult)
@@ -90,27 +107,19 @@ def tile_picked_yoit_over_p_kernel(tc, x_words, x_scales, w1, w2, depth, back, o
                 nc.tensor.transpose(bank[:, d, :], depth_scaled[:, c : c + 1].to_broadcast([P, P]), ident[:])
             depth_ps.append(bank)
 
-        picked_scales = keep.tile([P, S], U8, name="picked_scales", align_bytes=64)
-        nc.vector.tensor_copy(picked_scales[:], scale_table[:].indirect(offsets[:]))
-        x_scale = keep.tile([P, S], U8, name="x_scale", align_bytes=64)
-        nc.vector.tensor_copy(x_scale[:].bitcast(I32), picked_scales[:].bitcast(I32))
-        for o in range(PASSES):
-            for r in range(1, 4):
-                nc.scalar.dma_start(x_scale[4 * o + r : P : 32, :].bitcast(I32), picked_scales[8 * r + 4 * o : P : 32, :].bitcast(I32))
-        x0 = keep.tile([P, S], U32, name="x0", tag="scale_table", align_bytes=64)
+        x0 = keep.tile([P, S], U32, name="x0", align_bytes=64)
         nc.vector.tensor_copy(x0[:], word_tables[0][:].bitcast(U32).indirect(offsets[:]))
-        back_sb = keep.tile([P, V], F32, name="back_sb", tag="picked_scales", align_bytes=64)
-        nc.sync.dma_start(back_sb[:], back)
+        w1_raw0 = load_pass(w1, 0, "w1_raw0", "word_table0")
         x1 = [keep.tile([P, SH], U32, name="x1_%d" % h, align_bytes=64) for h in range(HALVES)]
 
         def product(bank, wq, o, h):
-            codes, scales = wq
+            codes, scales = wq[o]
             cols = slice(h * SH, (h + 1) * SH)
             moving = x0[:, cols] if o == 0 else x1[h][:]
             nc.tensor.matmul_mx(
                 out=bank[:],
-                lhsT=codes[:, o * N : (o + 1) * N].bitcast(FP8X4),
-                lhsT_scale=scales[:, o * N : (o + 1) * N],
+                lhsT=codes[:].bitcast(FP8X4),
+                lhsT_scale=scales[:],
                 rhs=moving.bitcast(FP8X4),
                 rhs_scale=x_scale[4 * o : P, cols],
                 start=(o == 0),
@@ -122,29 +131,24 @@ def tile_picked_yoit_over_p_kernel(tc, x_words, x_scales, w1, w2, depth, back, o
         for h in range(HALVES):
             product(z_ps[h], w2_q, 0, h)
 
-        one = keep.tile([P, 1], F32, name="one", tag="sig1")
-        nc.gpsimd.memset(one[:], 1.0)
-        sig, passing = [], []
+        sig = []
         for h in range(HALVES):
             nc.vector.tensor_copy(x1[h][:], word_tables[1][:].bitcast(U32).indirect(offsets[:, h * SH // 16 : (h + 1) * SH // 16]))
             product(z_ps[h], w2_q, 1, h)
-        w1_q = quantise(w1_raw, "w1")
+        w1_q = [quantise(w1_raw0, "w1_0"), w1_q1]
+        back_sb = keep.tile([P, V], F32, name="back_sb", tag="word_table0", align_bytes=64)
+        nc.sync.dma_start(back_sb[:], back)
         for h in range(HALVES):
             s = keep.tile([P, D, VH], F32, name="sig%d" % h)
             nc.scalar.activation(s[:], z_ps[h][:].rearrange("p (v d) -> p d v", d=D), ACT.Sigmoid)
             sig.append(s)
-            u = keep.tile([P, D, VH], F32, name="u%d" % h)
-            if h == 0:
-                nc.scalar.activation(u[:], s[:], ACT.Identity, scale=-0.95, bias=one[:])
-            passing.append(u)
         for h in range(HALVES):
             for o in range(PASSES):
                 product(col_ps[h], w1_q, o, h)
         tr = keep.tile([P, V], F32, name="tr")
         for h in range(HALVES):
-            u = passing[h]
-            if h == 1:
-                nc.gpsimd.tensor_scalar(u[:], sig[h][:], -0.95, 1.0, ALU.mult, ALU.add)
+            u = keep.tile([P, D, VH], F32, name="u%d" % h, tag="u")
+            nc.gpsimd.tensor_scalar(u[:], sig[h][:], -0.95, 1.0, ALU.mult, ALU.add)
             pair = keep.tile([P, 2, VH], F32, name="pair%d" % h)
             nc.gpsimd.tensor_tensor(pair[:], u[:, 0:2, :], u[:, 2:4, :], ALU.mult)
             nc.gpsimd.tensor_tensor(tr[:, h * VH : (h + 1) * VH], pair[:, 0, :], pair[:, 1, :], ALU.mult)
@@ -168,7 +172,7 @@ def tile_picked_yoit_over_p_kernel(tc, x_words, x_scales, w1, w2, depth, back, o
 
         root = keep.tile([P, HALVES, N], F32, name="root")
         for h in range(HALVES):
-            nc.scalar.activation(root[:, h, :], den_ps[:, h, :], ACT.Abs_reciprocal_sqrt, bias=0.05)
+            nc.scalar.activation(root[:, h, :], den_ps[:, h, :], ACT.Abs_reciprocal_sqrt, bias=floor[:])
         inv_abs = keep.tile([P, HALVES, N], F32, name="inv_abs")
         for h in range(HALVES):
             nc.scalar.activation(inv_abs[:, h, :], root[:, h, :], ACT.Square)

@@ -43,8 +43,8 @@ def tile_picked_yoit_over_p_kernel(tc, x_words, x_scales, w1, w2, depth, back, o
         nc.gpsimd.memset(warm[:, 0:1], 0.0)
         nc.scalar.activation(warm[:, 1:2], warm[:, 0:1], ACT.Sigmoid)
 
-        depth_cols = keep.tile([P, HALVES, D], F32, name="depth_cols")
-        nc.sync.dma_start(depth_cols[:], depth[0, :].rearrange("(h v d) -> v h d", h=HALVES, d=D))
+        depth_rows = keep.tile([P, P], F32, name="depth_rows")
+        nc.vector.memset(depth_rows[:], 0.0)
 
         unit = keep.tile([P, 1], F32, name="unit", tag="word_table0", align_bytes=64)
         nc.gpsimd.memset(unit[:], 1.0)
@@ -66,6 +66,8 @@ def tile_picked_yoit_over_p_kernel(tc, x_words, x_scales, w1, w2, depth, back, o
 
         for o in range(PASSES):
             nc.sync.dma_start(scale_table[4 * o : P : 8, :].bitcast(I32), x_scales[o].bitcast(I32))
+
+        nc.sync.dma_start(depth_rows[0 : S // P, :], depth[0, :].rearrange("(r c) -> r c", c=P))
 
         def load_words(o, tag):
             table = keep.tile([P, T], I32, name="word_table%d" % o, tag=tag, align_bytes=64)
@@ -97,14 +99,16 @@ def tile_picked_yoit_over_p_kernel(tc, x_words, x_scales, w1, w2, depth, back, o
             for r in range(1, 4):
                 nc.sync.dma_start(x_scale[4 * o + r : P : 32, :].bitcast(I32), picked_scales[8 * r + 4 * o : P : 32, :].bitcast(I32))
 
-        depth_scaled = keep.tile([P, HALVES * D], F32, name="depth_scaled")
-        nc.vector.tensor_scalar(depth_scaled[:], depth_cols[:].rearrange("p h d -> p (h d)"), 0.95, None, ALU.mult)
+        depth_turned = psum.tile([P, P], F32, name="depth_turned", tag="den_ps")
+        nc.tensor.transpose(depth_turned[:], depth_rows[:], ident[:])
+        depth_scaled = keep.tile([P, S // P], F32, name="depth_scaled")
+        nc.vector.tensor_scalar(depth_scaled[:], depth_turned[:, 0 : S // P], 0.95, None, ALU.mult)
         depth_ps = []
         for h in range(HALVES):
-            bank = psum.tile([P, D, VH], F32, name="depth_ps%d" % h)
-            for d in range(D):
-                c = h * D + d
-                nc.tensor.transpose(bank[:, d, :], depth_scaled[:, c : c + 1].to_broadcast([P, P]), ident[:])
+            bank = psum.tile([P, SH], F32, name="depth_ps%d" % h)
+            for c in range(SH // P):
+                r = h * SH // P + c
+                nc.tensor.transpose(bank[:, c * P : (c + 1) * P], depth_scaled[:, r : r + 1].to_broadcast([P, P]), ident[:])
             depth_ps.append(bank)
 
         x0 = keep.tile([P, S], U32, name="x0", align_bytes=64)
@@ -145,13 +149,13 @@ def tile_picked_yoit_over_p_kernel(tc, x_words, x_scales, w1, w2, depth, back, o
         for h in range(HALVES):
             for o in range(PASSES):
                 product(col_ps[h], w1_q, o, h)
-        tr = keep.tile([P, V], F32, name="tr")
+        pairs = keep.tile([P, HALVES, 2, VH], F32, name="pairs")
         for h in range(HALVES):
             u = keep.tile([P, D, VH], F32, name="u%d" % h, tag="u")
             nc.gpsimd.tensor_scalar(u[:], sig[h][:], -0.95, 1.0, ALU.mult, ALU.add)
-            pair = keep.tile([P, 2, VH], F32, name="pair%d" % h)
-            nc.gpsimd.tensor_tensor(pair[:], u[:, 0:2, :], u[:, 2:4, :], ALU.mult)
-            nc.gpsimd.tensor_tensor(tr[:, h * VH : (h + 1) * VH], pair[:, 0, :], pair[:, 1, :], ALU.mult)
+            nc.gpsimd.tensor_tensor(pairs[:, h], u[:, 0:2, :], u[:, 2:4, :], ALU.mult)
+        tr = keep.tile([P, V], F32, name="tr")
+        nc.gpsimd.tensor_tensor(tr[:].rearrange("p (h v) -> p h v", h=HALVES), pairs[:, :, 0, :], pairs[:, :, 1, :], ALU.mult)
 
         def sum_turned(bank, terms):
             for d in range(D):
@@ -162,7 +166,7 @@ def tile_picked_yoit_over_p_kernel(tc, x_words, x_scales, w1, w2, depth, back, o
         den_ps = psum.tile([P, HALVES, N], F32, name="den_ps")
         num_ps = []
         for h in range(HALVES):
-            nc.vector.tensor_tensor(ww[h][:], sig[h][:], depth_ps[h][:], ALU.mult)
+            nc.vector.tensor_tensor(ww[h][:], sig[h][:], depth_ps[h][:].rearrange("p (v d) -> p d v", d=D), ALU.mult)
             sum_turned(den_ps[:, h, :], ww[h])
         for h in range(HALVES):
             nc.vector.tensor_tensor(cw[h][:], ww[h][:], col_ps[h][:].rearrange("p (v d) -> p d v", d=D), ALU.mult)

from contextlib import ExitStack

import concourse.mybir as mybir
from concourse.masks import make_identity

K, T, S, D, N, V = 1024, 4096, 1024, 4, 128, 256
FLOPS = 2 * 2 * K * N * S
BYTES = K * T + (K // 32) * T + 2 * K * N * 4 + S * 4 + 2 * N * V * 4 + 128 * (S // 16) * 2

F32 = mybir.dt.float32
BF16 = mybir.dt.bfloat16
I32 = mybir.dt.int32
U32 = mybir.dt.uint32
U16 = mybir.dt.uint16
U8 = mybir.dt.uint8
FP8X4 = mybir.dt.float8_e4m3fn_x4
ACT = mybir.ActivationFunctionType
ALU = mybir.AluOpType
AX = mybir.AxisListType

P = 128
PACK = 4
PASSES = K // (P * PACK)
HALVES = 2
SH = S // HALVES
VH = V // HALVES


def tile_picked_yoit_over_p_kernel(tc, x_words, x_scales, w1, w2, depth, back, offs, out):
    nc = tc.nc
    with ExitStack() as ctx:
        keep = ctx.enter_context(tc.tile_pool(name="keep", bufs=1))
        psum = ctx.enter_context(tc.psum_pool(name="psum", bufs=1))

        offsets = keep.tile([P, S // 16], U16, name="offsets")
        nc.sync.dma_start(offsets[:], offs)

        scale_table = keep.tile([P, T], U8, name="scale_table", align_bytes=64)
        nc.gpsimd.memset(scale_table[:, : T // 2].bitcast(I32), 0)
        nc.vector.memset(scale_table[:, T // 2 :].bitcast(I32), 0)

        warm = keep.tile([P, 2], F32, name="warm")
        nc.gpsimd.memset(warm[:, 0:1], 0.0)
        nc.scalar.activation(warm[:, 1:2], warm[:, 0:1], ACT.Sigmoid)

        depth_rows = keep.tile([P, P], F32, name="depth_rows")
        nc.vector.memset(depth_rows[:], 0.0)

        unit = keep.tile([P, 1], F32, name="unit", tag="word_table0", align_bytes=64)
        nc.gpsimd.memset(unit[:], 1.0)
        floor = keep.tile([P, 1], F32, name="floor")
        nc.vector.tensor_scalar(floor[:], unit[:], 0.05, None, ALU.mult)

        def load_weight(w, name, tag):
            both = keep.tile([P, PASSES, PACK, N], F32, name=name, tag=tag, align_bytes=64)
            nc.sync.dma_start(both[:], w.rearrange("(o p j) m -> p o j m", o=PASSES, j=PACK))
            return [both[:, o] for o in range(PASSES)]

        def load_pass(w, o, name, tag):
            raw = keep.tile([P, PACK, N], F32, name=name, tag=tag, align_bytes=64)
            nc.sync.dma_start(raw[:], w[512 * o : 512 * (o + 1), :].rearrange("(p j) m -> p j m", j=PACK))
            return raw[:]

        w2_raw = load_weight(w2, "w2_both", "w2_both")
        w1_raw1 = load_pass(w1, 1, "w1_raw1", "w1_raw1")

        for o in range(PASSES):
            nc.sync.dma_start(scale_table[4 * o : P : 8, :].bitcast(I32), x_scales[o].bitcast(I32))

        nc.sync.dma_start(depth_rows[0 : S // P, :], depth[0, :].rearrange("(r c) -> r c", c=P))

        def load_words(o, tag):
            table = keep.tile([P, T], I32, name="word_table%d" % o, tag=tag, align_bytes=64)
            nc.sync.dma_start(table[:], x_words[o].rearrange("p n t -> p (n t)").bitcast(I32))
            return table

        word_tables = [load_words(0, "word_table0")]

        ident = keep.tile([P, P], F32, name="ident")
        make_identity(nc, ident[:])

        def quantise(raw, name):
            grouped = keep.tile([P, N, PACK], BF16, name=name + "_bf16", align_bytes=64)
            nc.scalar.copy(grouped[:], raw.rearrange("p j m -> p m j"))
            codes = keep.tile([P, N], U32, name=name + "_codes", align_bytes=64)
            scales = keep.tile([P, N], U8, name=name + "_scales", align_bytes=64)
            nc.vector.quantize_mx(out=codes[:].bitcast(FP8X4), scales=scales[:], in_=grouped[:].rearrange("p m j -> p (m j)"))
            return codes, scales

        w2_q = [quantise(w2_raw[o], "w2_%d" % o) for o in range(PASSES)]
        w1_q1 = quantise(w1_raw1, "w1_1")
        word_tables.append(load_words(1, "w2_both"))

        picked_scales = keep.tile([P, S], U8, name="picked_scales", align_bytes=64)
        nc.vector.tensor_copy(picked_scales[:], scale_table[:].indirect(offsets[:]))
        x_scale = keep.tile([P, S], U8, name="x_scale", align_bytes=64)
        nc.vector.tensor_copy(x_scale[:].bitcast(I32), picked_scales[:].bitcast(I32))
        for o in range(PASSES):
            for r in range(1, 4):
                nc.sync.dma_start(x_scale[4 * o + r : P : 32, :].bitcast(I32), picked_scales[8 * r + 4 * o : P : 32, :].bitcast(I32))

        depth_turned = psum.tile([P, P], F32, name="depth_turned", tag="den_ps")
        nc.tensor.transpose(depth_turned[:], depth_rows[:], ident[:])
        depth_scaled = keep.tile([P, S // P], F32, name="depth_scaled")
        nc.vector.tensor_scalar(depth_scaled[:], depth_turned[:, 0 : S // P], 0.95, None, ALU.mult)
        depth_ps = []
        for h in range(HALVES):
            bank = psum.tile([P, SH], F32, name="depth_ps%d" % h)
            for c in range(SH // P):
                r = h * SH // P + c
                nc.tensor.transpose(bank[:, c * P : (c + 1) * P], depth_scaled[:, r : r + 1].to_broadcast([P, P]), ident[:])
            depth_ps.append(bank)

        x0 = keep.tile([P, S], U32, name="x0", align_bytes=64)
        nc.vector.tensor_copy(x0[:], word_tables[0][:].bitcast(U32).indirect(offsets[:]))
        w1_raw0 = load_pass(w1, 0, "w1_raw0", "word_table0")
        x1 = [keep.tile([P, SH], U32, name="x1_%d" % h, align_bytes=64) for h in range(HALVES)]

        def product(bank, wq, o, h):
            codes, scales = wq[o]
            cols = slice(h * SH, (h + 1) * SH)
            moving = x0[:, cols] if o == 0 else x1[h][:]
            nc.tensor.matmul_mx(
                out=bank[:],
                lhsT=codes[:].bitcast(FP8X4),
                lhsT_scale=scales[:],
                rhs=moving.bitcast(FP8X4),
                rhs_scale=x_scale[4 * o : P, cols],
                start=(o == 0),
                stop=(o == PASSES - 1),
            )

        z_ps = [psum.tile([P, SH], F32, name="z_ps%d" % h) for h in range(HALVES)]
        col_ps = [psum.tile([P, SH], F32, name="col_ps%d" % h) for h in range(HALVES)]
        for h in range(HALVES):
            product(z_ps[h], w2_q, 0, h)

        sig = []
        for h in range(HALVES):
            nc.vector.tensor_copy(x1[h][:], word_tables[1][:].bitcast(U32).indirect(offsets[:, h * SH // 16 : (h + 1) * SH // 16]))
            product(z_ps[h], w2_q, 1, h)
        w1_q = [quantise(w1_raw0, "w1_0"), w1_q1]
        back_sb = keep.tile([P, V], F32, name="back_sb", tag="word_table0", align_bytes=64)
        nc.sync.dma_start(back_sb[:], back)
        for h in range(HALVES):
            s = keep.tile([P, D, VH], F32, name="sig%d" % h)
            nc.scalar.activation(s[:], z_ps[h][:].rearrange("p (v d) -> p d v", d=D), ACT.Sigmoid)
            sig.append(s)
        for h in range(HALVES):
            for o in range(PASSES):
                product(col_ps[h], w1_q, o, h)
        pairs = keep.tile([P, HALVES, 2, VH], F32, name="pairs")
        for h in range(HALVES):
            u = keep.tile([P, D, VH], F32, name="u%d" % h, tag="u")
            nc.gpsimd.tensor_scalar(u[:], sig[h][:], -0.95, 1.0, ALU.mult, ALU.add)
            nc.gpsimd.tensor_tensor(pairs[:, h], u[:, 0:2, :], u[:, 2:4, :], ALU.mult)
        tr = keep.tile([P, V], F32, name="tr")
        nc.gpsimd.tensor_tensor(tr[:].rearrange("p (h v) -> p h v", h=HALVES), pairs[:, :, 0, :], pairs[:, :, 1, :], ALU.mult)

        def sum_turned(bank, terms):
            for d in range(D):
                nc.tensor.matmul(bank, lhsT=terms[:, d, :], rhs=ident[:], is_transpose=True, start=(d == 0), stop=(d == D - 1))

        ww = [keep.tile([P, D, VH], F32, name="ww%d" % h) for h in range(HALVES)]
        cw = [keep.tile([P, D, VH], F32, name="cw%d" % h) for h in range(HALVES)]
        den_ps = psum.tile([P, HALVES, N], F32, name="den_ps")
        num_ps = []
        for h in range(HALVES):
            nc.vector.tensor_tensor(ww[h][:], sig[h][:], depth_ps[h][:].rearrange("p (v d) -> p d v", d=D), ALU.mult)
            sum_turned(den_ps[:, h, :], ww[h])
        for h in range(HALVES):
            nc.vector.tensor_tensor(cw[h][:], ww[h][:], col_ps[h][:].rearrange("p (v d) -> p d v", d=D), ALU.mult)
            bank = psum.tile([P, N], F32, name="num_ps%d" % h, tag="depth_ps%d" % h)
            sum_turned(bank[:], cw[h])
            num_ps.append(bank)

        root = keep.tile([P, HALVES, N], F32, name="root")
        for h in range(HALVES):
            nc.scalar.activation(root[:, h, :], den_ps[:, h, :], ACT.Abs_reciprocal_sqrt, bias=floor[:])
        inv_abs = keep.tile([P, HALVES, N], F32, name="inv_abs")
        for h in range(HALVES):
            nc.scalar.activation(inv_abs[:, h, :], root[:, h, :], ACT.Square)
        side = keep.tile([P, HALVES, N], F32, name="side")
        nc.vector.tensor_scalar(side[:], den_ps[:], -0.05, 2.0, ALU.is_ge, ALU.mult)
        signed = keep.tile([P, HALVES, N], F32, name="signed")
        for h in range(HALVES):
            nc.vector.scalar_tensor_tensor(signed[:, h, :], side[:, h, :], 1.0, num_ps[h][:], ALU.subtract, ALU.mult)
        avg_ps = []
        for h in range(HALVES):
            avg_t = keep.tile([P, N], F32, name="avg_t%d" % h)
            nc.vector.tensor_tensor(avg_t[:], signed[:, h, :], inv_abs[:, h, :], ALU.mult)
            bank = psum.tile([P, VH], F32, name="avg_ps%d" % h, tag="z_ps%d" % h)
            nc.tensor.transpose(bank[:], avg_t[:], ident[:])
            avg_ps.append(bank)
        bt = keep.tile([P, V], F32, name="bt", tag="inv_abs")
        nc.vector.tensor_tensor(bt[:], tr[:], back_sb[:], ALU.mult)
        hidden = [keep.tile([P, VH], F32, name="hidden%d" % h) for h in range(HALVES)]
        for h in range(HALVES):
            nc.vector.scalar_tensor_tensor(hidden[h][:], tr[:, h * VH : (h + 1) * VH], 1.0, avg_ps[h][:], ALU.subtract, ALU.mult)
        for h in range(HALVES):
            res = keep.tile([P, VH], F32, name="res%d" % h)
            nc.vector.tensor_tensor(res[:], bt[:, h * VH : (h + 1) * VH], hidden[h][:], ALU.subtract)
            nc.sync.dma_start(out[:, h * VH : (h + 1) * VH], res[:])
